import numpy as np
import ml_dtypes


def mxq(x, axis, fmt="e4m3"):
    dtype, down = {"e4m3": (ml_dtypes.float8_e4m3fn, 7), "e5m2": (ml_dtypes.float8_e5m2, 14)}[fmt]
    v = np.moveaxis(np.asarray(x, np.float32).astype(ml_dtypes.bfloat16).astype(np.float64), axis, -1)
    blocks = v.reshape(v.shape[:-1] + (-1, 32))
    amax = np.abs(blocks).max(-1, keepdims=True)
    byte = np.maximum(np.where(amax > 0, np.frexp(amax)[1] - 1 + 127, 0) - down, 1)
    scale = np.exp2(byte - 127.0)
    codes = (blocks / scale).astype(np.float32).astype(dtype).astype(np.float64)
    return np.moveaxis((codes * scale).reshape(v.shape), -1, axis)


WIDE = False


def mx_kscale(k):
    if not WIDE:
        return np.ones(k)
    levels = np.array([10, -10, 5, -5, 0])
    if k % 512:
        return np.exp2(np.random.permutation(np.resize(levels, k // 32))).repeat(32)
    a = np.empty((k // 512, 16))
    for p in range(k // 512):
        a[p, :8] = np.random.permutation(np.resize(levels, 8))
        for g in range(8):
            far = levels[np.abs(levels - a[p, g]) >= 10]
            a[p, g + 8] = far[np.random.randint(len(far))]
    return np.exp2(a.ravel()).repeat(32)


def f64(x):
    return np.asarray(x).astype(np.float64)


def striped(idx):
    return np.tile(idx.reshape(-1, 16).T, (8, 1)).astype(np.uint16)


def unstriped(offs):
    return offs[:16].T.reshape(-1).astype(np.int64)


def pack_weight(w):
    k, n = w.shape
    w = f64(np.asarray(w, np.float32).astype(ml_dtypes.bfloat16)).reshape(k // 32, 32, n)
    amax = np.abs(w).max(1)
    byte = np.clip(np.where(amax > 0, np.frexp(amax)[1] - 1 + 127 - 7, 1), 1, 254)
    scaled = (w * np.exp2(127.0 - byte)[:, None, :]).reshape(k, n).astype(np.float32)
    words = np.ascontiguousarray(scaled.reshape(k // 512, 128, 4, n).transpose(0, 1, 3, 2)).astype(ml_dtypes.float8_e4m3fn).view(np.uint8)
    return words, np.ascontiguousarray(byte.astype(np.uint8).reshape(k // 512, 16, n))


def unpack_weight(words, scales):
    g, p, n, _ = words.shape
    vals = np.ascontiguousarray(words).view(ml_dtypes.float8_e4m3fn).astype(np.float64) * np.repeat(np.exp2(scales.astype(np.float64) - 127.0), 8, axis=1)[..., None]
    return vals.transpose(0, 1, 3, 2).reshape(g * 512, n)


def relu(v):
    return np.maximum(v, 0.0)

def planes(y):
    n, m = y.shape
    v = y.astype(np.float32).astype(ml_dtypes.bfloat16).astype(np.float64).reshape(n // 32, 32, m)
    top = np.abs(v).max(1)
    byte = np.clip(np.where(top > 0, np.frexp(top)[1] - 1 + 127 - 7, 1), 1, 254)
    codes = (v * np.exp2(127.0 - byte)[:, None, :]).reshape(n, m).astype(np.float32).astype(ml_dtypes.float8_e4m3fn).view(np.uint8)
    words = codes.reshape(n // 512, 128, 4, m).transpose(0, 1, 3, 2)
    return np.ascontiguousarray(words), np.ascontiguousarray(byte.astype(np.uint8).reshape(n // 512, 16, m))


K, T, S, V, H = 512, 1024, 512, 256, 512


def setup_inputs():
    n = np.random.standard_normal
    s = mx_kscale(K)[:, None]
    u = mx_kscale(H)
    packed_xT = pack_weight(n((K, T)) * s)
    return {
        "x_words": packed_xT[0],
        "x_scales": packed_xT[1],
        "w1": (n((K, H)) / np.sqrt(2 * K) / s * u).astype(np.float32),
        "w2": (n((K, H)) / np.sqrt(2 * K) / s * u).astype(np.float32),
        "w3": (n((H, H)) / np.sqrt(H) / u[:, None]).astype(np.float32),
        "offs": striped(np.random.permutation(T)[:S]),
        "cen": striped(np.random.permutation(S)[:V]),
        "pos1": striped(np.random.permutation(S)[:V]),
        "pos2": striped(np.random.permutation(S)[:V]),
        "pos3": striped(np.random.permutation(S)[:V]),
        "pos4": striped(np.random.permutation(S)[:V]),
    }


def reference(x_words, x_scales, w1, w2, w3, offs, cen, pos1, pos2, pos3, pos4):
    xq = unpack_weight(x_words, x_scales)[:, unstriped(offs)]
    y = mxq(f64(w1), 0, "e4m3").T @ xq
    yc = y[:, unstriped(cen)]
    e = mxq(f64(w2), 0, "e4m3").T @ xq
    z = np.maximum(np.maximum(np.maximum(relu(yc + e[:, unstriped(pos1)]), relu(yc + e[:, unstriped(pos2)])), relu(yc + e[:, unstriped(pos3)])), relu(yc + e[:, unstriped(pos4)]))
    out_0 = mxq(f64(w3), 0, "e4m3").T @ mxq(z, 0, "e4m3")
    return (out_0,) + planes(out_0)

@@ -1,0 +1,243 @@
+from contextlib import ExitStack
+
+import concourse.mybir as mybir
+
+K, T, S, V, H = 512, 1024, 512, 256, 512
+FLOPS = 2 * K * H * S * 2 + 2 * H * H * V
+
+F32 = mybir.dt.float32
+BF16 = mybir.dt.bfloat16
+I32 = mybir.dt.int32
+U32 = mybir.dt.uint32
+U16 = mybir.dt.uint16
+U8 = mybir.dt.uint8
+FP8X4 = mybir.dt.float8_e4m3fn_x4
+ALU = mybir.AluOpType
+COPY = mybir.ActivationFunctionType.Copy
+RELU = mybir.ActivationFunctionType.Relu
+
+P = 128
+PACK = 4
+RUN = 8
+HALF = V // 2
+
+
+def tile_picked_edgecv_relu_po_kernel(
+    tc, x_words, x_scales, w1, w2, w3, offs, cen, pos1, pos2, pos3, pos4, out_0, out_1, out_2
+):
+    nc = tc.nc
+    with ExitStack() as ctx:
+        keep = ctx.enter_context(tc.tile_pool(name="keep", bufs=1))
+        psum = ctx.enter_context(tc.psum_pool(name="psum", bufs=1))
+
+        def sb(name, shape, dtype):
+            return keep.tile(shape, dtype, name=name, align_bytes=64)
+
+        offs_t = keep.tile([P, S // 16], U16, name="offs_t")
+        cen_t = keep.tile([P, V // 16], U16, name="cen_t")
+        pos_t = [keep.tile([P, V // 16], U16, name="pos_t%d" % d) for d in range(4)]
+
+        xw = sb("xw", [P, T], U32)
+        xs = sb("xs", [P, T], U8)
+        w2_raw = [sb("w2_raw%d" % h, [P, PACK, H // 2], F32) for h in range(2)]
+        w1_raw = sb("w1_raw", [P, PACK, H], F32)
+        w3_raw = sb("w3_raw", [P, PACK, H], F32)
+
+        nc.vector.memset(xs[:].bitcast(I32), 0)
+        nc.sync.dma_start(offs_t[:], offs)
+        for q in range(4):
+            nc.scalar.dma_start(
+                out=xs[32 * q : 32 * q + 4, :].bitcast(I32), in_=x_scales[0, 4 * q : 4 * q + 4, :].bitcast(I32)
+            )
+        nc.sync.dma_start(out=xw[:].bitcast(I32), in_=x_words[0].rearrange("p n t -> p (n t)").bitcast(I32))
+        w2_rows = w2.rearrange("(p j) c -> p j c", j=PACK)
+        for h in range(2):
+            nc.sync.dma_start(out=w2_raw[h][:], in_=w2_rows[:, :, h * (H // 2) : (h + 1) * (H // 2)])
+        nc.sync.dma_start(out=w1_raw[:], in_=w1.rearrange("(p j) c -> p j c", j=PACK))
+        for d, pos in enumerate((pos1, pos2, pos3, pos4)):
+            nc.sync.dma_start(pos_t[d][:], pos)
+        nc.sync.dma_start(cen_t[:], cen)
+        w3_rows = w3.rearrange("(b j r) m -> j b r m", j=PACK, r=RUN)
+        for j in range(PACK):
+            nc.sync.dma_start(out=w3_raw[:, j, :], in_=w3_rows[j])
+
+        xg_s = sb("xg_s", [P, S], U8)
+        xg_w = sb("xg_w", [P, S], U32)
+        nc.vector.tensor_copy(xg_s[:], xs[:].indirect(offs_t[:]))
+        nc.vector.tensor_copy(xg_w[:], xw[:].indirect(offs_t[:]))
+
+        def copy_on(engine, out, in_):
+            if engine == "vector":
+                nc.vector.tensor_copy(out=out, in_=in_)
+            else:
+                nc.scalar.copy(out=out, in_=in_)
+
+        def round_columns(engine, out, raw, t):
+            copy_on(
+                engine,
+                out.rearrange("p (b r j) -> p b r j", r=RUN, j=PACK),
+                raw.rearrange("p j (b t r) -> p t b r j", t=PACK, r=RUN)[:, t],
+            )
+
+        def quantize(name, rounded, width):
+            codes = sb(name + "_codes", [P, width], U32)
+            scales = sb(name + "_scales", [P, width], U8)
+            nc.vector.quantize_mx(out=codes[:].bitcast(FP8X4), scales=scales[:], in_=rounded)
+            return codes, scales
+
+        def product(bank, codes, scales):
+            nc.tensor.matmul_mx(
+                out=bank[:],
+                lhsT=codes.bitcast(FP8X4),
+                lhsT_scale=scales,
+                rhs=xg_w[:].bitcast(FP8X4),
+                rhs_scale=xg_s[:],
+                start=True,
+                stop=True,
+            )
+
+        w2_b = [sb("w2_b%d" % t, [P, P * PACK], BF16) for t in range(PACK)]
+        for h in range(2):
+            for t in range(PACK):
+                engine = "vector" if t < 2 else "scalar"
+                round_columns(engine, w2_b[t][:, h * 256 : (h + 1) * 256], w2_raw[h][:], t)
+        e_bank = []
+        for t in range(PACK):
+            codes, scales = quantize("w2q%d" % t, w2_b[t][:], P)
+            bank = psum.tile([P, S], F32, name="e_bank%d" % t, tag="bank%d" % t)
+            product(bank, codes[:], scales[:])
+            e_bank.append(bank)
+
+        e_sb = [sb("e_sb%d" % t, [P, S], F32) for t in range(PACK)]
+        y_sb = [sb("y_sb%d" % t, [P, S], F32) for t in range(PACK)]
+        z = sb("z", [P, PACK, V], F32)
+
+        def gather(engine, out, window, offsets):
+            if engine == "vector":
+                nc.vector.tensor_copy(out, window.indirect(offsets))
+            else:
+                nc.scalar.activation(out, window.indirect(offsets), COPY)
+
+        pairs, twos, tops = {}, {}, {}
+
+        def fetch(engine, name, t, lo, n, d):
+            if name not in pairs:
+                pairs[name] = [sb("%s_pair%d" % (name, u), [P, 2, n], F32) for u in range(2)]
+            gather(engine, pairs[name][d // 2][:, d % 2, :], e_sb[t][:], pos_t[d][:, lo // 16 : (lo + n) // 16])
+
+        def four_to_two(name, n):
+            twos[name] = sb(name + "_two", [P, 2, n], F32)
+            nc.vector.tensor_tensor(twos[name][:], pairs[name][0][:], pairs[name][1][:], ALU.max)
+
+        def two_to_one(name, n):
+            tops[name] = sb(name + "_one", [P, n], F32)
+            nc.vector.tensor_tensor(tops[name][:], twos[name][:, 0, :], twos[name][:, 1, :], ALU.max)
+
+        def add_centre(name, t, lo, n):
+            nc.vector.tensor_tensor(
+                z[:, t, lo : lo + n], y_sb[t][:].indirect(cen_t[:, lo // 16 : (lo + n) // 16]), tops[name][:], ALU.add
+            )
+
+        copy_on("scalar", e_sb[0][:], e_bank[0][:])
+        copy_on("vector", e_sb[1][:], e_bank[1][:])
+        for d in range(4):
+            fetch("scalar", "n0", 0, 0, V, d)
+
+        w1_b = sb("w1_b", [P, PACK, P * PACK], BF16)
+        for t in range(PACK):
+            round_columns("vector", w1_b[:, t, :], w1_raw[:], t)
+        fetch("vector", "n1", 1, 0, V, 0)
+        w1_codes, w1_scales = quantize("w1q", w1_b[:].rearrange("p t c -> p (t c)"), H)
+        y_bank = []
+        for t in range(PACK):
+            bank = psum.tile([P, S], F32, name="y_bank%d" % t, tag="bank%d" % (PACK + t))
+            product(bank, w1_codes[:, t * P : (t + 1) * P], w1_scales[:, t * P : (t + 1) * P])
+            y_bank.append(bank)
+        for d in range(1, 4):
+            fetch("vector", "n1", 1, 0, V, d)
+
+        copy_on("scalar", e_sb[2][:], e_bank[2][:])
+        for d in range(4):
+            fetch("scalar", "n2", 2, 0, V, d)
+        copy_on("scalar", e_sb[3][:], e_bank[3][:])
+        copy_on("scalar", y_sb[0][:], y_bank[0][:])
+        copy_on("scalar", y_sb[1][:], y_bank[1][:])
+        for d in range(4):
+            fetch("scalar", "n3a", 3, 0, HALF, d)
+        copy_on("scalar", y_sb[2][:], y_bank[2][:])
+        copy_on("scalar", y_sb[3][:], y_bank[3][:])
+        for d in range(4):
+            fetch("scalar", "n3b", 3, HALF, HALF, d)
+
+        four_to_two("n0", V)
+        four_to_two("n1", V)
+        two_to_one("n0", V)
+        two_to_one("n1", V)
+        four_to_two("n2", V)
+        add_centre("n0", 0, 0, V)
+        two_to_one("n2", V)
+        add_centre("n1", 1, 0, V)
+        four_to_two("n3a", HALF)
+
+        w3_b = sb("w3_b", [P, H * PACK], BF16)
+        w3_dealt = w3_b[:].rearrange("p (t m j) -> p m t j", t=PACK, j=PACK)
+        w3_src = w3_raw[:].rearrange("p j (m t) -> p m t j", t=PACK)
+        copy_on("vector", w3_dealt[:, : P // 2], w3_src[:, : P // 2])
+        copy_on("scalar", w3_dealt[:, P // 2 :], w3_src[:, P // 2 :])
+        two_to_one("n3a", HALF)
+        add_centre("n2", 2, 0, V)
+        add_centre("n3a", 3, 0, HALF)
+        four_to_two("n3b", HALF)
+        w3_codes, w3_scales = quantize("w3q", w3_b[:], H)
+        two_to_one("n3b", HALF)
+
+        o_codes = sb("o_codes", [P, V], U32)
+        o_scales = sb("o_scales", [P, V], U8)
+        out_rows = out_0.rearrange("(p t) v -> p t v", t=PACK)
+        z_b = [sb("z_b%d" % h, [P, HALF, PACK], BF16) for h in range(2)]
+        o_b = [sb("o_b%d" % h, [P, HALF, PACK], BF16) for h in range(2)]
+        o_sb = [sb("o_sb%d" % h, [P, PACK, HALF], F32) for h in range(2)]
+
+        def project(h):
+            z_codes, z_scales = quantize("zq%d" % h, z_b[h][:].rearrange("p v t -> p (v t)"), HALF)
+            bank = psum.tile([P, PACK, HALF], F32, name="o_bank%d" % h, tag="bank%d" % h)
+            for t in range(PACK):
+                nc.tensor.matmul_mx(
+                    out=bank[:, t, :],
+                    lhsT=w3_codes[:, t * P : (t + 1) * P].bitcast(FP8X4),
+                    lhsT_scale=w3_scales[:, t * P : (t + 1) * P],
+                    rhs=z_codes[:].bitcast(FP8X4),
+                    rhs_scale=z_scales[:],
+                    start=True,
+                    stop=True,
+                )
+            return bank
+
+        def quantize_out(h):
+            nc.vector.quantize_mx(
+                out=o_codes[:, h * HALF : (h + 1) * HALF].bitcast(FP8X4),
+                scales=o_scales[:, h * HALF : (h + 1) * HALF],
+                in_=o_b[h][:].rearrange("p v t -> p (v t)"),
+            )
+
+        nc.scalar.activation(z_b[0][:], z[:, :, :HALF].rearrange("p t v -> p v t"), RELU)
+        bank0 = project(0)
+        add_centre("n3b", 3, HALF, HALF)
+        nc.vector.tensor_scalar(
+            out=z_b[1][:], in0=z[:, :, HALF:].rearrange("p t v -> p v t"), scalar1=0.0, scalar2=None, op0=ALU.max
+        )
+        bank1 = project(1)
+        nc.scalar.copy(out=o_sb[0][:], in_=bank0[:])
+        nc.sync.dma_start(out=out_rows[:, :, :HALF], in_=o_sb[0][:])
+        nc.scalar.copy(out=o_b[0][:], in_=o_sb[0][:].rearrange("p t v -> p v t"))
+        quantize_out(0)
+        nc.vector.tensor_copy(out=o_b[1][:], in_=bank1[:].rearrange("p t v -> p v t"))
+        nc.scalar.copy(out=o_sb[1][:], in_=bank1[:])
+        nc.scalar.dma_start(out=out_rows[:, :, HALF:], in_=o_sb[1][:])
+        quantize_out(1)
+        nc.sync.dma_start(out=out_1[0].rearrange("p n t -> p (n t)").bitcast(I32), in_=o_codes[:].bitcast(I32))
+        for q in range(4):
+            queue = nc.sync if q < 2 else nc.scalar
+            queue.dma_start(
+                out=out_2[0, 4 * q : 4 * q + 4, :].bitcast(I32), in_=o_scales[32 * q : 32 * q + 4, :].bitcast(I32)
+            )

@@ -39,20 +39,21 @@ def tile_picked_edgecv_relu_po_kernel(
 
         xw = sb("xw", [P, T], U32)
         xs = sb("xs", [P, T], U8)
-        w2_raw = [sb("w2_raw%d" % h, [P, PACK, H // 2], F32) for h in range(2)]
+        w2_raw = [sb("w2_raw%d" % u, [P, 2, H], F32) for u in range(2)]
         w1_raw = sb("w1_raw", [P, PACK, H], F32)
         w3_raw = sb("w3_raw", [P, PACK, H], F32)
 
-        nc.vector.memset(xs[:].bitcast(I32), 0)
         nc.sync.dma_start(offs_t[:], offs)
         for q in range(4):
-            nc.scalar.dma_start(
-                out=xs[32 * q : 32 * q + 4, :].bitcast(I32), in_=x_scales[0, 4 * q : 4 * q + 4, :].bitcast(I32)
+            queue = nc.sync if q < 2 else nc.scalar
+            queue.dma_start(
+                out=xs[32 * q : 32 * q + 32, :].bitcast(I32),
+                in_=x_scales[0, 4 * q : 4 * q + 4, :].bitcast(I32).rearrange("r c -> (r c)").partition_broadcast(8),
             )
         nc.sync.dma_start(out=xw[:].bitcast(I32), in_=x_words[0].rearrange("p n t -> p (n t)").bitcast(I32))
         w2_rows = w2.rearrange("(p j) c -> p j c", j=PACK)
-        for h in range(2):
-            nc.sync.dma_start(out=w2_raw[h][:], in_=w2_rows[:, :, h * (H // 2) : (h + 1) * (H // 2)])
+        for u in range(2):
+            nc.sync.dma_start(out=w2_raw[u][:], in_=w2_rows[:, 2 * u : 2 * u + 2, :])
         nc.sync.dma_start(out=w1_raw[:], in_=w1.rearrange("(p j) c -> p j c", j=PACK))
         for d, pos in enumerate((pos1, pos2, pos3, pos4)):
             nc.sync.dma_start(pos_t[d][:], pos)
@@ -75,9 +76,12 @@ def tile_picked_edgecv_relu_po_kernel(
         def round_columns(engine, out, raw, t):
             copy_on(
                 engine,
-                out.rearrange("p (b r j) -> p b r j", r=RUN, j=PACK),
-                raw.rearrange("p j (b t r) -> p t b r j", t=PACK, r=RUN)[:, t],
+                out.rearrange("p (b r i) j -> p b r j i", r=2, i=4),
+                raw.rearrange("p j (b t r i) -> p t b r j i", t=PACK, r=2, i=4)[:, t],
             )
+
+        def weave(src, dst):
+            return src.rearrange("p t (c i) -> p c t i", i=4), dst.rearrange("p (c i) t -> p c t i", i=4)
 
         def quantize(name, rounded, width):
             codes = sb(name + "_codes", [P, width], U32)
@@ -85,28 +89,32 @@ def tile_picked_edgecv_relu_po_kernel(
             nc.vector.quantize_mx(out=codes[:].bitcast(FP8X4), scales=scales[:], in_=rounded)
             return codes, scales
 
-        def product(bank, codes, scales):
+        def product(bank, codes, scales, cols):
             nc.tensor.matmul_mx(
                 out=bank[:],
                 lhsT=codes.bitcast(FP8X4),
                 lhsT_scale=scales,
-                rhs=xg_w[:].bitcast(FP8X4),
-                rhs_scale=xg_s[:],
+                rhs=xg_w[:, cols].bitcast(FP8X4),
+                rhs_scale=xg_s[:, cols],
                 start=True,
                 stop=True,
             )
 
-        w2_b = [sb("w2_b%d" % t, [P, P * PACK], BF16) for t in range(PACK)]
-        for h in range(2):
+        w2_b = [sb("w2_b%d" % t, [P, P, PACK], BF16) for t in range(PACK)]
+        for u in range(2):
             for t in range(PACK):
-                engine = "vector" if t < 2 else "scalar"
-                round_columns(engine, w2_b[t][:, h * 256 : (h + 1) * 256], w2_raw[h][:], t)
-        e_bank = []
+                engine = "vector" if u == 1 and t < 2 else "scalar"
+                round_columns(engine, w2_b[t][:, :, 2 * u : 2 * u + 2], w2_raw[u][:], t)
+        e_bank = {}
         for t in range(PACK):
-            codes, scales = quantize("w2q%d" % t, w2_b[t][:], P)
-            bank = psum.tile([P, S], F32, name="e_bank%d" % t, tag="bank%d" % t)
-            product(bank, codes[:], scales[:])
-            e_bank.append(bank)
+            codes, scales = quantize("w2q%d" % t, w2_b[t][:].rearrange("p c j -> p (c j)"), P)
+            if t == 0:
+                for h in range(2):
+                    e_bank[t, h] = psum.tile([P, S // 2], F32, name="e_bank0%d" % h, tag="bank%d" % (7 * h))
+                    product(e_bank[t, h], codes[:], scales[:], slice(h * S // 2, (h + 1) * S // 2))
+            else:
+                e_bank[t] = psum.tile([P, S], F32, name="e_bank%d" % t, tag="bank%d" % t)
+                product(e_bank[t], codes[:], scales[:], slice(0, S))
 
         e_sb = [sb("e_sb%d" % t, [P, S], F32) for t in range(PACK)]
         y_sb = [sb("y_sb%d" % t, [P, S], F32) for t in range(PACK)]
@@ -138,28 +146,31 @@ def tile_picked_edgecv_relu_po_kernel(
                 z[:, t, lo : lo + n], y_sb[t][:].indirect(cen_t[:, lo // 16 : (lo + n) // 16]), tops[name][:], ALU.add
             )
 
-        copy_on("scalar", e_sb[0][:], e_bank[0][:])
+        copy_on("scalar", e_sb[0][:, : S // 2], e_bank[0, 0][:])
+        copy_on("vector", e_sb[0][:, S // 2 :], e_bank[0, 1][:])
         copy_on("vector", e_sb[1][:], e_bank[1][:])
-        for d in range(4):
+        for d in range(3):
             fetch("scalar", "n0", 0, 0, V, d)
+        copy_on("scalar", e_sb[2][:], e_bank[2][:])
+        fetch("scalar", "n0", 0, 0, V, 3)
 
-        w1_b = sb("w1_b", [P, PACK, P * PACK], BF16)
+        w1_b = sb("w1_b", [P, PACK, P, PACK], BF16)
         for t in range(PACK):
-            round_columns("vector", w1_b[:, t, :], w1_raw[:], t)
+            round_columns("vector", w1_b[:, t], w1_raw[:], t)
         fetch("vector", "n1", 1, 0, V, 0)
-        w1_codes, w1_scales = quantize("w1q", w1_b[:].rearrange("p t c -> p (t c)"), H)
+        w1_codes, w1_scales = quantize("w1q", w1_b[:].rearrange("p t c j -> p (t c j)"), H)
         y_bank = []
         for t in range(PACK):
             bank = psum.tile([P, S], F32, name="y_bank%d" % t, tag="bank%d" % (PACK + t))
-            product(bank, w1_codes[:, t * P : (t + 1) * P], w1_scales[:, t * P : (t + 1) * P])
+            product(bank, w1_codes[:, t * P : (t + 1) * P], w1_scales[:, t * P : (t + 1) * P], slice(0, S))
             y_bank.append(bank)
         for d in range(1, 4):
             fetch("vector", "n1", 1, 0, V, d)
 
-        copy_on("scalar", e_sb[2][:], e_bank[2][:])
-        for d in range(4):
+        for d in range(3):
             fetch("scalar", "n2", 2, 0, V, d)
         copy_on("scalar", e_sb[3][:], e_bank[3][:])
+        fetch("scalar", "n2", 2, 0, V, 3)
         copy_on("scalar", y_sb[0][:], y_bank[0][:])
         copy_on("scalar", y_sb[1][:], y_bank[1][:])
         for d in range(4):
@@ -180,8 +191,8 @@ def tile_picked_edgecv_relu_po_kernel(
         four_to_two("n3a", HALF)
 
         w3_b = sb("w3_b", [P, H * PACK], BF16)
-        w3_dealt = w3_b[:].rearrange("p (t m j) -> p m t j", t=PACK, j=PACK)
-        w3_src = w3_raw[:].rearrange("p j (m t) -> p m t j", t=PACK)
+        w3_dealt = w3_b[:].rearrange("p (t m j) -> p m j t", t=PACK, j=PACK)
+        w3_src = w3_raw[:].rearrange("p j (m t) -> p m j t", t=PACK)
         copy_on("vector", w3_dealt[:, : P // 2], w3_src[:, : P // 2])
         copy_on("scalar", w3_dealt[:, P // 2 :], w3_src[:, P // 2 :])
         two_to_one("n3a", HALF)
@@ -200,10 +211,10 @@ def tile_picked_edgecv_relu_po_kernel(
 
         def project(h):
             z_codes, z_scales = quantize("zq%d" % h, z_b[h][:].rearrange("p v t -> p (v t)"), HALF)
-            bank = psum.tile([P, PACK, HALF], F32, name="o_bank%d" % h, tag="bank%d" % h)
+            banks = [psum.tile([P, 2, HALF], F32, name="o_bank%d%d" % (h, u), tag="bank%d" % (2 * h + u)) for u in range(2)]
             for t in range(PACK):
                 nc.tensor.matmul_mx(
-                    out=bank[:, t, :],
+                    out=banks[t // 2][:, t % 2, :],
                     lhsT=w3_codes[:, t * P : (t + 1) * P].bitcast(FP8X4),
                     lhsT_scale=w3_scales[:, t * P : (t + 1) * P],
                     rhs=z_codes[:].bitcast(FP8X4),
@@ -211,7 +222,7 @@ def tile_picked_edgecv_relu_po_kernel(
                     start=True,
                     stop=True,
                 )
-            return bank
+            return banks
 
         def quantize_out(h):
             nc.vector.quantize_mx(
@@ -220,20 +231,24 @@ def tile_picked_edgecv_relu_po_kernel(
                 in_=o_b[h][:].rearrange("p v t -> p (v t)"),
             )
 
-        nc.scalar.activation(z_b[0][:], z[:, :, :HALF].rearrange("p t v -> p v t"), RELU)
-        bank0 = project(0)
+        src, dst = weave(z[:, :, :HALF], z_b[0][:])
+        nc.scalar.activation(dst, src, RELU)
+        banks0 = project(0)
         add_centre("n3b", 3, HALF, HALF)
-        nc.vector.tensor_scalar(
-            out=z_b[1][:], in0=z[:, :, HALF:].rearrange("p t v -> p v t"), scalar1=0.0, scalar2=None, op0=ALU.max
-        )
-        bank1 = project(1)
-        nc.scalar.copy(out=o_sb[0][:], in_=bank0[:])
+        src, dst = weave(z[:, :, HALF:], z_b[1][:])
+        nc.vector.tensor_scalar(out=dst, in0=src, scalar1=0.0, scalar2=None, op0=ALU.max)
+        banks1 = project(1)
+        for u in range(2):
+            copy_on("scalar", o_sb[0][:, 2 * u : 2 * u + 2, :], banks0[u][:])
         nc.sync.dma_start(out=out_rows[:, :, :HALF], in_=o_sb[0][:])
-        nc.scalar.copy(out=o_b[0][:], in_=o_sb[0][:].rearrange("p t v -> p v t"))
+        src, dst = weave(o_sb[0][:], o_b[0][:])
+        copy_on("vector", dst, src)
         quantize_out(0)
-        nc.vector.tensor_copy(out=o_b[1][:], in_=bank1[:].rearrange("p t v -> p v t"))
-        nc.scalar.copy(out=o_sb[1][:], in_=bank1[:])
+        copy_on("scalar", o_sb[1][:, 0:2, :], banks1[0][:])
+        copy_on("vector", o_sb[1][:, 2:4, :], banks1[1][:])
         nc.scalar.dma_start(out=out_rows[:, :, HALF:], in_=o_sb[1][:])
+        src, dst = weave(o_sb[1][:], o_b[1][:])
+        copy_on("vector", dst, src)
         quantize_out(1)
         nc.sync.dma_start(out=out_1[0].rearrange("p n t -> p (n t)").bitcast(I32), in_=o_codes[:].bitcast(I32))
         for q in range(4):

@@ -30,8 +30,8 @@ def tile_picked_edgecv_relu_po_kernel(
         keep = ctx.enter_context(tc.tile_pool(name="keep", bufs=1))
         psum = ctx.enter_context(tc.psum_pool(name="psum", bufs=1))
 
-        def sb(name, shape, dtype):
-            return keep.tile(shape, dtype, name=name, align_bytes=64)
+        def sb(name, shape, dtype, tag=None):
+            return keep.tile(shape, dtype, name=name, tag=tag or name, align_bytes=64)
 
         offs_t = keep.tile([P, S // 16], U16, name="offs_t")
         cen_t = keep.tile([P, V // 16], U16, name="cen_t")
@@ -54,9 +54,9 @@ def tile_picked_edgecv_relu_po_kernel(
         w2_rows = w2.rearrange("(p j) c -> p j c", j=PACK)
         for u in range(2):
             nc.sync.dma_start(out=w2_raw[u][:], in_=w2_rows[:, 2 * u : 2 * u + 2, :])
-        nc.sync.dma_start(out=w1_raw[:], in_=w1.rearrange("(p j) c -> p j c", j=PACK))
         for d, pos in enumerate((pos1, pos2, pos3, pos4)):
             nc.sync.dma_start(pos_t[d][:], pos)
+        nc.sync.dma_start(out=w1_raw[:], in_=w1.rearrange("(p j) c -> p j c", j=PACK))
         nc.sync.dma_start(cen_t[:], cen)
         w3_rows = w3.rearrange("(b j r) m -> j b r m", j=PACK, r=RUN)
         for j in range(PACK):
@@ -116,9 +116,9 @@ def tile_picked_edgecv_relu_po_kernel(
                 e_bank[t] = psum.tile([P, S], F32, name="e_bank%d" % t, tag="bank%d" % t)
                 product(e_bank[t], codes[:], scales[:], slice(0, S))
 
-        e_sb = [sb("e_sb%d" % t, [P, S], F32) for t in range(PACK)]
+        e_sb = [sb("e_sb%d" % t, [P, S], F32) for t in range(PACK - 1)]
         y_sb = [sb("y_sb%d" % t, [P, S], F32) for t in range(PACK)]
-        z = sb("z", [P, PACK, V], F32)
+        z = [sb("z%d" % h, [P, PACK, HALF], F32) for h in range(2)]
 
         def gather(engine, out, window, offsets):
             if engine == "vector":
@@ -126,81 +126,103 @@ def tile_picked_edgecv_relu_po_kernel(
             else:
                 nc.scalar.activation(out, window.indirect(offsets), COPY)
 
-        pairs, twos, tops = {}, {}, {}
+        def group(name, tiles, lo, n, slot):
+            pairs = [sb("%s_pair%d" % (name, u), [P, len(tiles), 2, n], F32, tag="pair%d%d" % (slot, u)) for u in range(2)]
+            return {"name": name, "tiles": tiles, "lo": lo, "n": n, "pairs": pairs}
 
-        def fetch(engine, name, t, lo, n, d):
-            if name not in pairs:
-                pairs[name] = [sb("%s_pair%d" % (name, u), [P, 2, n], F32) for u in range(2)]
-            gather(engine, pairs[name][d // 2][:, d % 2, :], e_sb[t][:], pos_t[d][:, lo // 16 : (lo + n) // 16])
-
-        def four_to_two(name, n):
-            twos[name] = sb(name + "_two", [P, 2, n], F32)
-            nc.vector.tensor_tensor(twos[name][:], pairs[name][0][:], pairs[name][1][:], ALU.max)
-
-        def two_to_one(name, n):
-            tops[name] = sb(name + "_one", [P, n], F32)
-            nc.vector.tensor_tensor(tops[name][:], twos[name][:, 0, :], twos[name][:, 1, :], ALU.max)
-
-        def add_centre(name, t, lo, n):
-            nc.vector.tensor_tensor(
-                z[:, t, lo : lo + n], y_sb[t][:].indirect(cen_t[:, lo // 16 : (lo + n) // 16]), tops[name][:], ALU.add
+        def fetch(engine, grp, k, d):
+            lo, n = grp["lo"], grp["n"]
+            gather(
+                engine,
+                grp["pairs"][d // 2][:, k, d % 2, :],
+                e_sb[grp["tiles"][k]][:],
+                pos_t[d][:, lo // 16 : (lo + n) // 16],
             )
+
+        def four_to_two(grp, tag=None):
+            two = sb(grp["name"] + "_two", [P, len(grp["tiles"]), 2, grp["n"]], F32, tag=tag)
+            nc.vector.tensor_tensor(two[:], grp["pairs"][0][:], grp["pairs"][1][:], ALU.max)
+            return two
+
+        def two_to_one(grp, two):
+            top = sb(grp["name"] + "_top", [P, len(grp["tiles"]), grp["n"]], F32)
+            nc.vector.tensor_tensor(top[:], two[:, :, 0, :], two[:, :, 1, :], ALU.max)
+            return top
+
+        def add_centre(grp, k, top, lo, n):
+            t, first = grp["tiles"][k], lo - grp["lo"]
+            nc.vector.tensor_tensor(
+                z[lo // HALF][:, t, :],
+                y_sb[t][:].indirect(cen_t[:, lo // 16 : (lo + n) // 16]),
+                top[:, k, first : first + n],
+                ALU.add,
+            )
+
+        g01 = group("g01", (0, 1), 0, V, 0)
+        g2 = group("g2", (2,), 0, V, 1)
+        g3a = group("g3a", (3,), 0, HALF, 2)
 
         copy_on("scalar", e_sb[0][:, : S // 2], e_bank[0, 0][:])
         copy_on("vector", e_sb[0][:, S // 2 :], e_bank[0, 1][:])
         copy_on("vector", e_sb[1][:], e_bank[1][:])
         for d in range(3):
-            fetch("scalar", "n0", 0, 0, V, d)
+            fetch("scalar", g01, 0, d)
         copy_on("scalar", e_sb[2][:], e_bank[2][:])
-        fetch("scalar", "n0", 0, 0, V, 3)
+        fetch("scalar", g01, 0, 3)
 
-        w1_b = sb("w1_b", [P, PACK, P, PACK], BF16)
+        w1_b = [sb("w1_b%d" % h, [P, 2, P, PACK], BF16) for h in range(2)]
         for t in range(PACK):
-            round_columns("vector", w1_b[:, t], w1_raw[:], t)
-        fetch("vector", "n1", 1, 0, V, 0)
-        w1_codes, w1_scales = quantize("w1q", w1_b[:].rearrange("p t c j -> p (t c j)"), H)
+            nc.gpsimd.tensor_scalar(
+                out=w1_b[t // 2][:, t % 2].rearrange("p (b r) j -> p b r j", r=RUN),
+                in0=w1_raw[:].rearrange("p j (b t r) -> p t b r j", t=PACK, r=RUN)[:, t],
+                scalar1=1.0,
+                scalar2=0.0,
+                op0=ALU.mult,
+                op1=ALU.add,
+            )
+        for d in range(4):
+            fetch("vector", g01, 1, d)
         y_bank = []
-        for t in range(PACK):
-            bank = psum.tile([P, S], F32, name="y_bank%d" % t, tag="bank%d" % (PACK + t))
-            product(bank, w1_codes[:, t * P : (t + 1) * P], w1_scales[:, t * P : (t + 1) * P], slice(0, S))
-            y_bank.append(bank)
-        for d in range(1, 4):
-            fetch("vector", "n1", 1, 0, V, d)
+        for h in range(2):
+            codes, scales = quantize("w1q%d" % h, w1_b[h][:].rearrange("p t c j -> p (t c j)"), 2 * P)
+            for k in range(2):
+                t = 2 * h + k
+                bank = psum.tile([P, S], F32, name="y_bank%d" % t, tag="bank%d" % (PACK + t))
+                product(bank, codes[:, k * P : (k + 1) * P], scales[:, k * P : (k + 1) * P], slice(0, S))
+                y_bank.append(bank)
 
         for d in range(3):
-            fetch("scalar", "n2", 2, 0, V, d)
+            fetch("scalar", g2, 0, d)
+        e_sb.append(sb("e_sb3", [P, S], F32, tag="w1_b0"))
         copy_on("scalar", e_sb[3][:], e_bank[3][:])
-        fetch("scalar", "n2", 2, 0, V, 3)
-        copy_on("scalar", y_sb[0][:], y_bank[0][:])
-        copy_on("scalar", y_sb[1][:], y_bank[1][:])
+        fetch("scalar", g2, 0, 3)
+        for t in range(2):
+            copy_on("scalar", y_sb[t][:], y_bank[t][:])
         for d in range(4):
-            fetch("scalar", "n3a", 3, 0, HALF, d)
-        copy_on("scalar", y_sb[2][:], y_bank[2][:])
-        copy_on("scalar", y_sb[3][:], y_bank[3][:])
-        for d in range(4):
-            fetch("scalar", "n3b", 3, HALF, HALF, d)
+            fetch("scalar", g3a, 0, d)
+        for t in range(2, PACK):
+            copy_on("scalar", y_sb[t][:], y_bank[t][:])
 
-        four_to_two("n0", V)
-        four_to_two("n1", V)
-        two_to_one("n0", V)
-        two_to_one("n1", V)
-        four_to_two("n2", V)
-        add_centre("n0", 0, 0, V)
-        two_to_one("n2", V)
-        add_centre("n1", 1, 0, V)
-        four_to_two("n3a", HALF)
-
-        w3_b = sb("w3_b", [P, H * PACK], BF16)
+        w3_b = sb("w3_b", [P, H * PACK], BF16, tag="w1_b1")
         w3_dealt = w3_b[:].rearrange("p (t m j) -> p m j t", t=PACK, j=PACK)
         w3_src = w3_raw[:].rearrange("p j (m t) -> p m j t", t=PACK)
+        two01 = four_to_two(g01, "w1_raw")
         copy_on("vector", w3_dealt[:, : P // 2], w3_src[:, : P // 2])
-        copy_on("scalar", w3_dealt[:, P // 2 :], w3_src[:, P // 2 :])
-        two_to_one("n3a", HALF)
-        add_centre("n2", 2, 0, V)
-        add_centre("n3a", 3, 0, HALF)
-        four_to_two("n3b", HALF)
+        top01 = two_to_one(g01, two01)
+        copy_on("vector", w3_dealt[:, P // 2 :], w3_src[:, P // 2 :])
+        two2 = four_to_two(g2, "pair00")
+        g3b = group("g3b", (3,), HALF, HALF, 1)
+        for d in range(2):
+            fetch("scalar", g3b, 0, d)
         w3_codes, w3_scales = quantize("w3q", w3_b[:], H)
-        two_to_one("n3b", HALF)
+        top2 = two_to_one(g2, two2)
+        add_centre(g01, 0, top01, 0, HALF)
+        add_centre(g01, 0, top01, HALF, HALF)
+        two3a = four_to_two(g3a)
+        add_centre(g01, 1, top01, 0, HALF)
+        top3a = two_to_one(g3a, two3a)
+        add_centre(g2, 0, top2, 0, HALF)
+        add_centre(g3a, 0, top3a, 0, HALF)
 
         o_codes = sb("o_codes", [P, V], U32)
         o_scales = sb("o_scales", [P, V], U8)
@@ -231,19 +253,25 @@ def tile_picked_edgecv_relu_po_kernel(
                 in_=o_b[h][:].rearrange("p v t -> p (v t)"),
             )
 
-        src, dst = weave(z[:, :, :HALF], z_b[0][:])
+        src, dst = weave(z[0][:], z_b[0][:])
         nc.scalar.activation(dst, src, RELU)
+        for d in range(2, 4):
+            fetch("scalar", g3b, 0, d)
+        add_centre(g01, 1, top01, HALF, HALF)
+        add_centre(g2, 0, top2, HALF, HALF)
         banks0 = project(0)
-        add_centre("n3b", 3, HALF, HALF)
-        src, dst = weave(z[:, :, HALF:], z_b[1][:])
-        nc.vector.tensor_scalar(out=dst, in0=src, scalar1=0.0, scalar2=None, op0=ALU.max)
-        banks1 = project(1)
+        two3b = four_to_two(g3b)
+        top3b = two_to_one(g3b, two3b)
+        add_centre(g3b, 0, top3b, HALF, HALF)
         for u in range(2):
             copy_on("scalar", o_sb[0][:, 2 * u : 2 * u + 2, :], banks0[u][:])
         nc.sync.dma_start(out=out_rows[:, :, :HALF], in_=o_sb[0][:])
         src, dst = weave(o_sb[0][:], o_b[0][:])
-        copy_on("vector", dst, src)
+        copy_on("scalar", dst, src)
+        src, dst = weave(z[1][:], z_b[1][:])
+        nc.vector.tensor_scalar(out=dst, in0=src, scalar1=0.0, scalar2=None, op0=ALU.max)
         quantize_out(0)
+        banks1 = project(1)
         copy_on("scalar", o_sb[1][:, 0:2, :], banks1[0][:])
         copy_on("vector", o_sb[1][:, 2:4, :], banks1[1][:])
         nc.scalar.dma_start(out=out_rows[:, :, HALF:], in_=o_sb[1][:])

@@ -20,6 +20,7 @@ P = 128
 PACK = 4
 RUN = 8
 HALF = V // 2
+QUARTER = V // 4
 
 
 def tile_picked_edgecv_relu_po_kernel(
@@ -152,7 +153,7 @@ def tile_picked_edgecv_relu_po_kernel(
         def add_centre(grp, k, top, lo, n):
             t, first = grp["tiles"][k], lo - grp["lo"]
             nc.vector.tensor_tensor(
-                z[lo // HALF][:, t, :],
+                z[lo // HALF][:, t, lo % HALF : lo % HALF + n],
                 y_sb[t][:].indirect(cen_t[:, lo // 16 : (lo + n) // 16]),
                 top[:, k, first : first + n],
                 ALU.add,
@@ -171,25 +172,19 @@ def tile_picked_edgecv_relu_po_kernel(
         fetch("scalar", g01, 0, 3)
 
         w1_b = [sb("w1_b%d" % h, [P, 2, P, PACK], BF16) for h in range(2)]
-        for t in range(PACK):
-            nc.gpsimd.tensor_scalar(
-                out=w1_b[t // 2][:, t % 2].rearrange("p (b r) j -> p b r j", r=RUN),
-                in0=w1_raw[:].rearrange("p j (b t r) -> p t b r j", t=PACK, r=RUN)[:, t],
-                scalar1=1.0,
-                scalar2=0.0,
-                op0=ALU.mult,
-                op1=ALU.add,
-            )
-        for d in range(4):
-            fetch("vector", g01, 1, d)
         y_bank = []
         for h in range(2):
+            for k in range(2):
+                round_columns("vector", w1_b[h][:, k], w1_raw[:], 2 * h + k)
+            fetch("vector", g01, 1, h)
             codes, scales = quantize("w1q%d" % h, w1_b[h][:].rearrange("p t c j -> p (t c j)"), 2 * P)
             for k in range(2):
                 t = 2 * h + k
                 bank = psum.tile([P, S], F32, name="y_bank%d" % t, tag="bank%d" % (PACK + t))
                 product(bank, codes[:, k * P : (k + 1) * P], scales[:, k * P : (k + 1) * P], slice(0, S))
                 y_bank.append(bank)
+        fetch("vector", g01, 1, 2)
+        fetch("scalar", g01, 1, 3)
 
         for d in range(3):
             fetch("scalar", g2, 0, d)
@@ -212,7 +207,7 @@ def tile_picked_edgecv_relu_po_kernel(
         copy_on("vector", w3_dealt[:, P // 2 :], w3_src[:, P // 2 :])
         two2 = four_to_two(g2, "pair00")
         g3b = group("g3b", (3,), HALF, HALF, 1)
-        for d in range(2):
+        for d in range(4):
             fetch("scalar", g3b, 0, d)
         w3_codes, w3_scales = quantize("w3q", w3_b[:], H)
         top2 = two_to_one(g2, two2)
@@ -227,12 +222,22 @@ def tile_picked_edgecv_relu_po_kernel(
         o_codes = sb("o_codes", [P, V], U32)
         o_scales = sb("o_scales", [P, V], U8)
         out_rows = out_0.rearrange("(p t) v -> p t v", t=PACK)
-        z_b = [sb("z_b%d" % h, [P, HALF, PACK], BF16) for h in range(2)]
-        o_b = [sb("o_b%d" % h, [P, HALF, PACK], BF16) for h in range(2)]
+        pieces = [(0, 0, HALF), (1, 0, QUARTER), (1, QUARTER, QUARTER)]
+        z_b = {(h, lo): sb("z_b%d_%d" % (h, lo), [P, n, PACK], BF16) for h, lo, n in pieces}
+        o_b = {(h, lo): sb("o_b%d_%d" % (h, lo), [P, n, PACK], BF16) for h, lo, n in pieces}
         o_sb = [sb("o_sb%d" % h, [P, PACK, HALF], F32) for h in range(2)]
 
+        z_q = [(sb("z_codes%d" % h, [P, HALF], U32), sb("z_scales%d" % h, [P, HALF], U8)) for h in range(2)]
+
+        def quantize_z(h, lo, n):
+            nc.vector.quantize_mx(
+                out=z_q[h][0][:, lo : lo + n].bitcast(FP8X4),
+                scales=z_q[h][1][:, lo : lo + n],
+                in_=z_b[h, lo][:].rearrange("p v t -> p (v t)"),
+            )
+
         def project(h):
-            z_codes, z_scales = quantize("zq%d" % h, z_b[h][:].rearrange("p v t -> p (v t)"), HALF)
+            z_codes, z_scales = z_q[h]
             banks = [psum.tile([P, 2, HALF], F32, name="o_bank%d%d" % (h, u), tag="bank%d" % (2 * h + u)) for u in range(2)]
             for t in range(PACK):
                 nc.tensor.matmul_mx(
@@ -246,38 +251,44 @@ def tile_picked_edgecv_relu_po_kernel(
                 )
             return banks
 
-        def quantize_out(h):
+        def quantize_out(h, lo, n):
             nc.vector.quantize_mx(
-                out=o_codes[:, h * HALF : (h + 1) * HALF].bitcast(FP8X4),
-                scales=o_scales[:, h * HALF : (h + 1) * HALF],
-                in_=o_b[h][:].rearrange("p v t -> p (v t)"),
+                out=o_codes[:, h * HALF + lo : h * HALF + lo + n].bitcast(FP8X4),
+                scales=o_scales[:, h * HALF + lo : h * HALF + lo + n],
+                in_=o_b[h, lo][:].rearrange("p v t -> p (v t)"),
             )
 
-        src, dst = weave(z[0][:], z_b[0][:])
+        src, dst = weave(z[0][:], z_b[0, 0][:])
         nc.scalar.activation(dst, src, RELU)
-        for d in range(2, 4):
-            fetch("scalar", g3b, 0, d)
         add_centre(g01, 1, top01, HALF, HALF)
         add_centre(g2, 0, top2, HALF, HALF)
-        banks0 = project(0)
         two3b = four_to_two(g3b)
+        quantize_z(0, 0, HALF)
+        banks0 = project(0)
         top3b = two_to_one(g3b, two3b)
-        add_centre(g3b, 0, top3b, HALF, HALF)
+        quarters = [q * QUARTER for q in range(2)]
+        for lo in quarters:
+            add_centre(g3b, 0, top3b, HALF + lo, QUARTER)
+        for lo in quarters:
+            src, dst = weave(z[1][:, :, lo : lo + QUARTER], z_b[1, lo][:])
+            nc.vector.tensor_scalar(out=dst, in0=src, scalar1=0.0, scalar2=None, op0=ALU.max)
+        for lo in quarters:
+            quantize_z(1, lo, QUARTER)
+        banks1 = project(1)
         for u in range(2):
             copy_on("scalar", o_sb[0][:, 2 * u : 2 * u + 2, :], banks0[u][:])
         nc.sync.dma_start(out=out_rows[:, :, :HALF], in_=o_sb[0][:])
-        src, dst = weave(o_sb[0][:], o_b[0][:])
-        copy_on("scalar", dst, src)
-        src, dst = weave(z[1][:], z_b[1][:])
-        nc.vector.tensor_scalar(out=dst, in0=src, scalar1=0.0, scalar2=None, op0=ALU.max)
-        quantize_out(0)
-        banks1 = project(1)
-        copy_on("scalar", o_sb[1][:, 0:2, :], banks1[0][:])
-        copy_on("vector", o_sb[1][:, 2:4, :], banks1[1][:])
-        nc.scalar.dma_start(out=out_rows[:, :, HALF:], in_=o_sb[1][:])
-        src, dst = weave(o_sb[1][:], o_b[1][:])
+        src, dst = weave(o_sb[0][:], o_b[0, 0][:])
         copy_on("vector", dst, src)
-        quantize_out(1)
+        quantize_out(0, 0, HALF)
+        for u in range(2):
+            copy_on("scalar", o_sb[1][:, 2 * u : 2 * u + 2, :], banks1[u][:])
+        nc.scalar.dma_start(out=out_rows[:, :, HALF:], in_=o_sb[1][:])
+        for lo in quarters:
+            src, dst = weave(o_sb[1][:, :, lo : lo + QUARTER], o_b[1, lo][:])
+            copy_on("vector", dst, src)
+        for lo in quarters:
+            quantize_out(1, lo, QUARTER)
         nc.sync.dma_start(out=out_1[0].rearrange("p n t -> p (n t)").bitcast(I32), in_=o_codes[:].bitcast(I32))
         for q in range(4):
             queue = nc.sync if q < 2 else nc.scalar

@@ -3,7 +3,7 @@ from contextlib import ExitStack
 import concourse.mybir as mybir
 
 K, T, S, V, H = 512, 1024, 512, 256, 512
-FLOPS = 2 * K * H * S * 2 + 2 * H * H * V
+FLOPS = 2 * (2 * K * H * S) + 2 * H * H * V
 
 F32 = mybir.dt.float32
 BF16 = mybir.dt.bfloat16
@@ -19,8 +19,13 @@ RELU = mybir.ActivationFunctionType.Relu
 P = 128
 PACK = 4
 RUN = 8
+WALK = 4
+LANES = 16
+QUADRANT = 32
+NEIGHBOURS = 4
 HALF = V // 2
 QUARTER = V // 4
+LAST_BANK = 7
 
 
 def tile_picked_edgecv_relu_po_kernel(
@@ -34,9 +39,9 @@ def tile_picked_edgecv_relu_po_kernel(
         def sb(name, shape, dtype, tag=None):
             return keep.tile(shape, dtype, name=name, tag=tag or name, align_bytes=64)
 
-        offs_t = keep.tile([P, S // 16], U16, name="offs_t")
-        cen_t = keep.tile([P, V // 16], U16, name="cen_t")
-        pos_t = [keep.tile([P, V // 16], U16, name="pos_t%d" % d) for d in range(4)]
+        offs_t = keep.tile([P, S // LANES], U16, name="offs_t")
+        cen_t = keep.tile([P, V // LANES], U16, name="cen_t")
+        pos_t = [keep.tile([P, V // LANES], U16, name="pos_t%d" % d) for d in range(NEIGHBOURS)]
 
         xw = sb("xw", [P, T], U32)
         xs = sb("xs", [P, T], U8)
@@ -44,14 +49,14 @@ def tile_picked_edgecv_relu_po_kernel(
         w1_raw = sb("w1_raw", [P, PACK, H], F32)
         w3_raw = sb("w3_raw", [P, PACK, H], F32)
 
+        nc.vector.memset(xs[:].bitcast(I32), 0)
         nc.sync.dma_start(offs_t[:], offs)
-        for q in range(4):
-            queue = nc.sync if q < 2 else nc.scalar
-            queue.dma_start(
-                out=xs[32 * q : 32 * q + 32, :].bitcast(I32),
-                in_=x_scales[0, 4 * q : 4 * q + 4, :].bitcast(I32).rearrange("r c -> (r c)").partition_broadcast(8),
-            )
         nc.sync.dma_start(out=xw[:].bitcast(I32), in_=x_words[0].rearrange("p n t -> p (n t)").bitcast(I32))
+        for q in range(P // QUADRANT):
+            nc.sync.dma_start(
+                out=xs[QUADRANT * q : QUADRANT * q + PACK, :].bitcast(I32),
+                in_=x_scales[0, PACK * q : PACK * (q + 1), :].bitcast(I32),
+            )
         w2_rows = w2.rearrange("(p j) c -> p j c", j=PACK)
         for u in range(2):
             nc.sync.dma_start(out=w2_raw[u][:], in_=w2_rows[:, 2 * u : 2 * u + 2, :])
@@ -65,8 +70,8 @@ def tile_picked_edgecv_relu_po_kernel(
 
         xg_s = sb("xg_s", [P, S], U8)
         xg_w = sb("xg_w", [P, S], U32)
-        nc.vector.tensor_copy(xg_s[:], xs[:].indirect(offs_t[:]))
         nc.vector.tensor_copy(xg_w[:], xw[:].indirect(offs_t[:]))
+        nc.vector.tensor_copy(xg_s[:], xs[:].indirect(offs_t[:]))
 
         def copy_on(engine, out, in_):
             if engine == "vector":
@@ -77,12 +82,12 @@ def tile_picked_edgecv_relu_po_kernel(
         def round_columns(engine, out, raw, t):
             copy_on(
                 engine,
-                out.rearrange("p (b r i) j -> p b r j i", r=2, i=4),
-                raw.rearrange("p j (b t r i) -> p t b r j i", t=PACK, r=2, i=4)[:, t],
+                out.rearrange("p (b r i) j -> p b r j i", r=RUN // WALK, i=WALK),
+                raw.rearrange("p j (b t r i) -> p t b r j i", t=PACK, r=RUN // WALK, i=WALK)[:, t],
             )
 
         def weave(src, dst):
-            return src.rearrange("p t (c i) -> p c t i", i=4), dst.rearrange("p (c i) t -> p c t i", i=4)
+            return src.rearrange("p t (c i) -> p c t i", i=WALK), dst.rearrange("p (c i) t -> p c t i", i=WALK)
 
         def quantize(name, rounded, width):
             codes = sb(name + "_codes", [P, width], U32)
@@ -111,7 +116,7 @@ def tile_picked_edgecv_relu_po_kernel(
             codes, scales = quantize("w2q%d" % t, w2_b[t][:].rearrange("p c j -> p (c j)"), P)
             if t == 0:
                 for h in range(2):
-                    e_bank[t, h] = psum.tile([P, S // 2], F32, name="e_bank0%d" % h, tag="bank%d" % (7 * h))
+                    e_bank[t, h] = psum.tile([P, S // 2], F32, name="e_bank0%d" % h, tag="bank%d" % (LAST_BANK * h))
                     product(e_bank[t, h], codes[:], scales[:], slice(h * S // 2, (h + 1) * S // 2))
             else:
                 e_bank[t] = psum.tile([P, S], F32, name="e_bank%d" % t, tag="bank%d" % t)
@@ -127,17 +132,19 @@ def tile_picked_edgecv_relu_po_kernel(
             else:
                 nc.scalar.activation(out, window.indirect(offsets), COPY)
 
-        def group(name, tiles, lo, n, slot):
-            pairs = [sb("%s_pair%d" % (name, u), [P, len(tiles), 2, n], F32, tag="pair%d%d" % (slot, u)) for u in range(2)]
+        def group(name, tiles, lo, n, buffer):
+            pairs = [
+                sb("%s_pair%d" % (name, u), [P, len(tiles), 2, n], F32, tag="pair%d%d" % (buffer, u)) for u in range(2)
+            ]
             return {"name": name, "tiles": tiles, "lo": lo, "n": n, "pairs": pairs}
 
-        def fetch(engine, grp, k, d):
+        def fetch(engine, grp, member, d):
             lo, n = grp["lo"], grp["n"]
             gather(
                 engine,
-                grp["pairs"][d // 2][:, k, d % 2, :],
-                e_sb[grp["tiles"][k]][:],
-                pos_t[d][:, lo // 16 : (lo + n) // 16],
+                grp["pairs"][d // 2][:, member, d % 2, :],
+                e_sb[grp["tiles"][member]][:],
+                pos_t[d][:, lo // LANES : (lo + n) // LANES],
             )
 
         def four_to_two(grp, tag=None):
@@ -150,12 +157,12 @@ def tile_picked_edgecv_relu_po_kernel(
             nc.vector.tensor_tensor(top[:], two[:, :, 0, :], two[:, :, 1, :], ALU.max)
             return top
 
-        def add_centre(grp, k, top, lo, n):
-            t, first = grp["tiles"][k], lo - grp["lo"]
+        def add_centre(grp, member, top, lo, n):
+            t, first = grp["tiles"][member], lo - grp["lo"]
             nc.vector.tensor_tensor(
                 z[lo // HALF][:, t, lo % HALF : lo % HALF + n],
-                y_sb[t][:].indirect(cen_t[:, lo // 16 : (lo + n) // 16]),
-                top[:, k, first : first + n],
+                y_sb[t][:].indirect(cen_t[:, lo // LANES : (lo + n) // LANES]),
+                top[:, member, first : first + n],
                 ALU.add,
             )
 
@@ -166,34 +173,34 @@ def tile_picked_edgecv_relu_po_kernel(
         copy_on("scalar", e_sb[0][:, : S // 2], e_bank[0, 0][:])
         copy_on("vector", e_sb[0][:, S // 2 :], e_bank[0, 1][:])
         copy_on("vector", e_sb[1][:], e_bank[1][:])
-        for d in range(3):
+        for d in range(NEIGHBOURS - 1):
             fetch("scalar", g01, 0, d)
         copy_on("scalar", e_sb[2][:], e_bank[2][:])
-        fetch("scalar", g01, 0, 3)
+        fetch("scalar", g01, 0, NEIGHBOURS - 1)
 
         w1_b = [sb("w1_b%d" % h, [P, 2, P, PACK], BF16) for h in range(2)]
         y_bank = []
         for h in range(2):
-            for k in range(2):
-                round_columns("vector", w1_b[h][:, k], w1_raw[:], 2 * h + k)
+            for a in range(2):
+                round_columns("vector", w1_b[h][:, a], w1_raw[:], 2 * h + a)
             fetch("vector", g01, 1, h)
             codes, scales = quantize("w1q%d" % h, w1_b[h][:].rearrange("p t c j -> p (t c j)"), 2 * P)
-            for k in range(2):
-                t = 2 * h + k
+            for a in range(2):
+                t = 2 * h + a
                 bank = psum.tile([P, S], F32, name="y_bank%d" % t, tag="bank%d" % (PACK + t))
-                product(bank, codes[:, k * P : (k + 1) * P], scales[:, k * P : (k + 1) * P], slice(0, S))
+                product(bank, codes[:, a * P : (a + 1) * P], scales[:, a * P : (a + 1) * P], slice(0, S))
                 y_bank.append(bank)
         fetch("vector", g01, 1, 2)
         fetch("scalar", g01, 1, 3)
 
-        for d in range(3):
+        for d in range(NEIGHBOURS - 1):
             fetch("scalar", g2, 0, d)
         e_sb.append(sb("e_sb3", [P, S], F32, tag="w1_b0"))
         copy_on("scalar", e_sb[3][:], e_bank[3][:])
-        fetch("scalar", g2, 0, 3)
+        fetch("scalar", g2, 0, NEIGHBOURS - 1)
         for t in range(2):
             copy_on("scalar", y_sb[t][:], y_bank[t][:])
-        for d in range(4):
+        for d in range(NEIGHBOURS):
             fetch("scalar", g3a, 0, d)
         for t in range(2, PACK):
             copy_on("scalar", y_sb[t][:], y_bank[t][:])
@@ -207,12 +214,11 @@ def tile_picked_edgecv_relu_po_kernel(
         copy_on("vector", w3_dealt[:, P // 2 :], w3_src[:, P // 2 :])
         two2 = four_to_two(g2, "pair00")
         g3b = group("g3b", (3,), HALF, HALF, 1)
-        for d in range(4):
+        for d in range(NEIGHBOURS - 1):
             fetch("scalar", g3b, 0, d)
         w3_codes, w3_scales = quantize("w3q", w3_b[:], H)
         top2 = two_to_one(g2, two2)
         add_centre(g01, 0, top01, 0, HALF)
-        add_centre(g01, 0, top01, HALF, HALF)
         two3a = four_to_two(g3a)
         add_centre(g01, 1, top01, 0, HALF)
         top3a = two_to_one(g3a, two3a)
@@ -238,7 +244,9 @@ def tile_picked_edgecv_relu_po_kernel(
 
         def project(h):
             z_codes, z_scales = z_q[h]
-            banks = [psum.tile([P, 2, HALF], F32, name="o_bank%d%d" % (h, u), tag="bank%d" % (2 * h + u)) for u in range(2)]
+            banks = [
+                psum.tile([P, 2, HALF], F32, name="o_bank%d%d" % (h, u), tag="bank%d" % (2 * h + u)) for u in range(2)
+            ]
             for t in range(PACK):
                 nc.tensor.matmul_mx(
                     out=banks[t // 2][:, t % 2, :],
@@ -261,11 +269,13 @@ def tile_picked_edgecv_relu_po_kernel(
         src, dst = weave(z[0][:], z_b[0, 0][:])
         nc.scalar.activation(dst, src, RELU)
         add_centre(g01, 1, top01, HALF, HALF)
+        fetch("vector", g3b, 0, NEIGHBOURS - 1)
         add_centre(g2, 0, top2, HALF, HALF)
         two3b = four_to_two(g3b)
         quantize_z(0, 0, HALF)
         banks0 = project(0)
         top3b = two_to_one(g3b, two3b)
+        add_centre(g01, 0, top01, HALF, HALF)
         quarters = [q * QUARTER for q in range(2)]
         for lo in quarters:
             add_centre(g3b, 0, top3b, HALF + lo, QUARTER)
@@ -275,12 +285,15 @@ def tile_picked_edgecv_relu_po_kernel(
         for lo in quarters:
             quantize_z(1, lo, QUARTER)
         banks1 = project(1)
+
         for u in range(2):
             copy_on("scalar", o_sb[0][:, 2 * u : 2 * u + 2, :], banks0[u][:])
         nc.sync.dma_start(out=out_rows[:, :, :HALF], in_=o_sb[0][:])
         src, dst = weave(o_sb[0][:], o_b[0, 0][:])
         copy_on("vector", dst, src)
         quantize_out(0, 0, HALF)
+        word_rows = out_1[0].rearrange("p n t -> p (n t)").bitcast(I32)
+        nc.sync.dma_start(out=word_rows[:, :HALF], in_=o_codes[:, :HALF].bitcast(I32))
         for u in range(2):
             copy_on("scalar", o_sb[1][:, 2 * u : 2 * u + 2, :], banks1[u][:])
         nc.scalar.dma_start(out=out_rows[:, :, HALF:], in_=o_sb[1][:])
@@ -289,9 +302,10 @@ def tile_picked_edgecv_relu_po_kernel(
             copy_on("vector", dst, src)
         for lo in quarters:
             quantize_out(1, lo, QUARTER)
-        nc.sync.dma_start(out=out_1[0].rearrange("p n t -> p (n t)").bitcast(I32), in_=o_codes[:].bitcast(I32))
-        for q in range(4):
+        nc.sync.dma_start(out=word_rows[:, HALF:], in_=o_codes[:, HALF:].bitcast(I32))
+        for q in range(P // QUADRANT):
             queue = nc.sync if q < 2 else nc.scalar
             queue.dma_start(
-                out=out_2[0, 4 * q : 4 * q + 4, :].bitcast(I32), in_=o_scales[32 * q : 32 * q + 4, :].bitcast(I32)
+                out=out_2[0, PACK * q : PACK * (q + 1), :].bitcast(I32),
+                in_=o_scales[QUADRANT * q : QUADRANT * q + PACK, :].bitcast(I32),
             )

from contextlib import ExitStack

import concourse.mybir as mybir

K, T, S, V, H = 512, 1024, 512, 256, 512
FLOPS = 2 * (2 * K * H * S) + 2 * H * H * V

F32 = mybir.dt.float32
BF16 = mybir.dt.bfloat16
I32 = mybir.dt.int32
U32 = mybir.dt.uint32
U16 = mybir.dt.uint16
U8 = mybir.dt.uint8
FP8X4 = mybir.dt.float8_e4m3fn_x4
ALU = mybir.AluOpType
COPY = mybir.ActivationFunctionType.Copy
RELU = mybir.ActivationFunctionType.Relu

P = 128
PACK = 4
RUN = 8
WALK = 4
LANES = 16
QUADRANT = 32
NEIGHBOURS = 4
HALF = V // 2
QUARTER = V // 4
LAST_BANK = 7


def tile_picked_edgecv_relu_po_kernel(
    tc, x_words, x_scales, w1, w2, w3, offs, cen, pos1, pos2, pos3, pos4, out_0, out_1, out_2
):
    nc = tc.nc
    with ExitStack() as ctx:
        keep = ctx.enter_context(tc.tile_pool(name="keep", bufs=1))
        psum = ctx.enter_context(tc.psum_pool(name="psum", bufs=1))

        def sb(name, shape, dtype, tag=None):
            return keep.tile(shape, dtype, name=name, tag=tag or name, align_bytes=64)

        offs_t = keep.tile([P, S // LANES], U16, name="offs_t")
        cen_t = keep.tile([P, V // LANES], U16, name="cen_t")
        pos_t = [keep.tile([P, V // LANES], U16, name="pos_t%d" % d) for d in range(NEIGHBOURS)]

        xw = sb("xw", [P, T], U32)
        xs = sb("xs", [P, T], U8)
        w2_raw = [sb("w2_raw%d" % u, [P, 2, H], F32) for u in range(2)]
        w1_raw = sb("w1_raw", [P, PACK, H], F32)
        w3_raw = sb("w3_raw", [P, PACK, H], F32)

        nc.vector.memset(xs[:].bitcast(I32), 0)
        nc.sync.dma_start(offs_t[:], offs)
        nc.sync.dma_start(out=xw[:].bitcast(I32), in_=x_words[0].rearrange("p n t -> p (n t)").bitcast(I32))
        for q in range(P // QUADRANT):
            nc.sync.dma_start(
                out=xs[QUADRANT * q : QUADRANT * q + PACK, :].bitcast(I32),
                in_=x_scales[0, PACK * q : PACK * (q + 1), :].bitcast(I32),
            )
        w2_rows = w2.rearrange("(p j) c -> p j c", j=PACK)
        for u in range(2):
            nc.sync.dma_start(out=w2_raw[u][:], in_=w2_rows[:, 2 * u : 2 * u + 2, :])
        for d, pos in enumerate((pos1, pos2, pos3, pos4)):
            nc.sync.dma_start(pos_t[d][:], pos)
        nc.sync.dma_start(out=w1_raw[:], in_=w1.rearrange("(p j) c -> p j c", j=PACK))
        nc.sync.dma_start(cen_t[:], cen)
        w3_rows = w3.rearrange("(b j r) m -> j b r m", j=PACK, r=RUN)
        for j in range(PACK):
            nc.sync.dma_start(out=w3_raw[:, j, :], in_=w3_rows[j])

        xg_s = sb("xg_s", [P, S], U8)
        xg_w = sb("xg_w", [P, S], U32)
        nc.vector.tensor_copy(xg_w[:], xw[:].indirect(offs_t[:]))
        nc.vector.tensor_copy(xg_s[:], xs[:].indirect(offs_t[:]))

        def copy_on(engine, out, in_):
            if engine == "vector":
                nc.vector.tensor_copy(out=out, in_=in_)
            else:
                nc.scalar.copy(out=out, in_=in_)

        def round_columns(engine, out, raw, t):
            copy_on(
                engine,
                out.rearrange("p (b r i) j -> p b r j i", r=RUN // WALK, i=WALK),
                raw.rearrange("p j (b t r i) -> p t b r j i", t=PACK, r=RUN // WALK, i=WALK)[:, t],
            )

        def weave(src, dst):
            return src.rearrange("p t (c i) -> p c t i", i=WALK), dst.rearrange("p (c i) t -> p c t i", i=WALK)

        def quantize(name, rounded, width):
            codes = sb(name + "_codes", [P, width], U32)
            scales = sb(name + "_scales", [P, width], U8)
            nc.vector.quantize_mx(out=codes[:].bitcast(FP8X4), scales=scales[:], in_=rounded)
            return codes, scales

        def product(bank, codes, scales, cols):
            nc.tensor.matmul_mx(
                out=bank[:],
                lhsT=codes.bitcast(FP8X4),
                lhsT_scale=scales,
                rhs=xg_w[:, cols].bitcast(FP8X4),
                rhs_scale=xg_s[:, cols],
                start=True,
                stop=True,
            )

        w2_b = [sb("w2_b%d" % t, [P, P, PACK], BF16) for t in range(PACK)]
        for u in range(2):
            for t in range(PACK):
                engine = "vector" if u == 1 and t < 2 else "scalar"
                round_columns(engine, w2_b[t][:, :, 2 * u : 2 * u + 2], w2_raw[u][:], t)
        e_bank = {}
        for t in range(PACK):
            codes, scales = quantize("w2q%d" % t, w2_b[t][:].rearrange("p c j -> p (c j)"), P)
            if t == 0:
                for h in range(2):
                    e_bank[t, h] = psum.tile([P, S // 2], F32, name="e_bank0%d" % h, tag="bank%d" % (LAST_BANK * h))
                    product(e_bank[t, h], codes[:], scales[:], slice(h * S // 2, (h + 1) * S // 2))
            else:
                e_bank[t] = psum.tile([P, S], F32, name="e_bank%d" % t, tag="bank%d" % t)
                product(e_bank[t], codes[:], scales[:], slice(0, S))

        e_sb = [sb("e_sb%d" % t, [P, S], F32) for t in range(PACK - 1)]
        y_sb = [sb("y_sb%d" % t, [P, S], F32) for t in range(PACK)]
        z = [sb("z%d" % h, [P, PACK, HALF], F32) for h in range(2)]

        def gather(engine, out, window, offsets):
            if engine == "vector":
                nc.vector.tensor_copy(out, window.indirect(offsets))
            else:
                nc.scalar.activation(out, window.indirect(offsets), COPY)

        def group(name, tiles, lo, n, buffer):
            pairs = [
                sb("%s_pair%d" % (name, u), [P, len(tiles), 2, n], F32, tag="pair%d%d" % (buffer, u)) for u in range(2)
            ]
            return {"name": name, "tiles": tiles, "lo": lo, "n": n, "pairs": pairs}

        def fetch(engine, grp, member, d):
            lo, n = grp["lo"], grp["n"]
            gather(
                engine,
                grp["pairs"][d // 2][:, member, d % 2, :],
                e_sb[grp["tiles"][member]][:],
                pos_t[d][:, lo // LANES : (lo + n) // LANES],
            )

        def four_to_two(grp, tag=None):
            two = sb(grp["name"] + "_two", [P, len(grp["tiles"]), 2, grp["n"]], F32, tag=tag)
            nc.vector.tensor_tensor(two[:], grp["pairs"][0][:], grp["pairs"][1][:], ALU.max)
            return two

        def two_to_one(grp, two):
            top = sb(grp["name"] + "_top", [P, len(grp["tiles"]), grp["n"]], F32)
            nc.vector.tensor_tensor(top[:], two[:, :, 0, :], two[:, :, 1, :], ALU.max)
            return top

        def add_centre(grp, member, top, lo, n):
            t, first = grp["tiles"][member], lo - grp["lo"]
            nc.vector.tensor_tensor(
                z[lo // HALF][:, t, lo % HALF : lo % HALF + n],
                y_sb[t][:].indirect(cen_t[:, lo // LANES : (lo + n) // LANES]),
                top[:, member, first : first + n],
                ALU.add,
            )

        g01 = group("g01", (0, 1), 0, V, 0)
        g2 = group("g2", (2,), 0, V, 1)
        g3a = group("g3a", (3,), 0, HALF, 2)

        copy_on("scalar", e_sb[0][:, : S // 2], e_bank[0, 0][:])
        copy_on("vector", e_sb[0][:, S // 2 :], e_bank[0, 1][:])
        copy_on("vector", e_sb[1][:], e_bank[1][:])
        for d in range(NEIGHBOURS - 1):
            fetch("scalar", g01, 0, d)
        copy_on("scalar", e_sb[2][:], e_bank[2][:])
        fetch("scalar", g01, 0, NEIGHBOURS - 1)

        w1_b = [sb("w1_b%d" % h, [P, 2, P, PACK], BF16) for h in range(2)]
        y_bank = []
        for h in range(2):
            for a in range(2):
                round_columns("vector", w1_b[h][:, a], w1_raw[:], 2 * h + a)
            fetch("vector", g01, 1, h)
            codes, scales = quantize("w1q%d" % h, w1_b[h][:].rearrange("p t c j -> p (t c j)"), 2 * P)
            for a in range(2):
                t = 2 * h + a
                bank = psum.tile([P, S], F32, name="y_bank%d" % t, tag="bank%d" % (PACK + t))
                product(bank, codes[:, a * P : (a + 1) * P], scales[:, a * P : (a + 1) * P], slice(0, S))
                y_bank.append(bank)
        fetch("vector", g01, 1, 2)
        fetch("scalar", g01, 1, 3)

        for d in range(NEIGHBOURS - 1):
            fetch("scalar", g2, 0, d)
        e_sb.append(sb("e_sb3", [P, S], F32, tag="w1_b0"))
        copy_on("scalar", e_sb[3][:], e_bank[3][:])
        fetch("scalar", g2, 0, NEIGHBOURS - 1)
        for t in range(2):
            copy_on("scalar", y_sb[t][:], y_bank[t][:])
        for d in range(NEIGHBOURS):
            fetch("scalar", g3a, 0, d)
        for t in range(2, PACK):
            copy_on("scalar", y_sb[t][:], y_bank[t][:])

        w3_b = sb("w3_b", [P, H * PACK], BF16, tag="w1_b1")
        w3_dealt = w3_b[:].rearrange("p (t m j) -> p m j t", t=PACK, j=PACK)
        w3_src = w3_raw[:].rearrange("p j (m t) -> p m j t", t=PACK)
        two01 = four_to_two(g01, "w1_raw")
        copy_on("vector", w3_dealt[:, : P // 2], w3_src[:, : P // 2])
        top01 = two_to_one(g01, two01)
        copy_on("vector", w3_dealt[:, P // 2 :], w3_src[:, P // 2 :])
        two2 = four_to_two(g2, "pair00")
        g3b = group("g3b", (3,), HALF, HALF, 1)
        for d in range(NEIGHBOURS - 1):
            fetch("scalar", g3b, 0, d)
        w3_codes, w3_scales = quantize("w3q", w3_b[:], H)
        top2 = two_to_one(g2, two2)
        add_centre(g01, 0, top01, 0, HALF)
        two3a = four_to_two(g3a)
        add_centre(g01, 1, top01, 0, HALF)
        top3a = two_to_one(g3a, two3a)
        add_centre(g2, 0, top2, 0, HALF)
        add_centre(g3a, 0, top3a, 0, HALF)

        o_codes = sb("o_codes", [P, V], U32)
        o_scales = sb("o_scales", [P, V], U8)
        out_rows = out_0.rearrange("(p t) v -> p t v", t=PACK)
        pieces = [(0, 0, HALF), (1, 0, QUARTER), (1, QUARTER, QUARTER)]
        z_b = {(h, lo): sb("z_b%d_%d" % (h, lo), [P, n, PACK], BF16) for h, lo, n in pieces}
        o_b = {(h, lo): sb("o_b%d_%d" % (h, lo), [P, n, PACK], BF16) for h, lo, n in pieces}
        o_sb = [sb("o_sb%d" % h, [P, PACK, HALF], F32) for h in range(2)]

        z_q = [(sb("z_codes%d" % h, [P, HALF], U32), sb("z_scales%d" % h, [P, HALF], U8)) for h in range(2)]

        def quantize_z(h, lo, n):
            nc.vector.quantize_mx(
                out=z_q[h][0][:, lo : lo + n].bitcast(FP8X4),
                scales=z_q[h][1][:, lo : lo + n],
                in_=z_b[h, lo][:].rearrange("p v t -> p (v t)"),
            )

        def project(h):
            z_codes, z_scales = z_q[h]
            banks = [
                psum.tile([P, 2, HALF], F32, name="o_bank%d%d" % (h, u), tag="bank%d" % (2 * h + u)) for u in range(2)
            ]
            for t in range(PACK):
                nc.tensor.matmul_mx(
                    out=banks[t // 2][:, t % 2, :],
                    lhsT=w3_codes[:, t * P : (t + 1) * P].bitcast(FP8X4),
                    lhsT_scale=w3_scales[:, t * P : (t + 1) * P],
                    rhs=z_codes[:].bitcast(FP8X4),
                    rhs_scale=z_scales[:],
                    start=True,
                    stop=True,
                )
            return banks

        def quantize_out(h, lo, n):
            nc.vector.quantize_mx(
                out=o_codes[:, h * HALF + lo : h * HALF + lo + n].bitcast(FP8X4),
                scales=o_scales[:, h * HALF + lo : h * HALF + lo + n],
                in_=o_b[h, lo][:].rearrange("p v t -> p (v t)"),
            )

        src, dst = weave(z[0][:], z_b[0, 0][:])
        nc.scalar.activation(dst, src, RELU)
        add_centre(g01, 1, top01, HALF, HALF)
        fetch("vector", g3b, 0, NEIGHBOURS - 1)
        add_centre(g2, 0, top2, HALF, HALF)
        two3b = four_to_two(g3b)
        quantize_z(0, 0, HALF)
        banks0 = project(0)
        top3b = two_to_one(g3b, two3b)
        add_centre(g01, 0, top01, HALF, HALF)
        quarters = [q * QUARTER for q in range(2)]
        for lo in quarters:
            add_centre(g3b, 0, top3b, HALF + lo, QUARTER)
        for lo in quarters:
            src, dst = weave(z[1][:, :, lo : lo + QUARTER], z_b[1, lo][:])
            nc.vector.tensor_scalar(out=dst, in0=src, scalar1=0.0, scalar2=None, op0=ALU.max)
        for lo in quarters:
            quantize_z(1, lo, QUARTER)
        banks1 = project(1)

        for u in range(2):
            copy_on("scalar", o_sb[0][:, 2 * u : 2 * u + 2, :], banks0[u][:])
        nc.sync.dma_start(out=out_rows[:, :, :HALF], in_=o_sb[0][:])
        src, dst = weave(o_sb[0][:], o_b[0, 0][:])
        copy_on("vector", dst, src)
        quantize_out(0, 0, HALF)
        word_rows = out_1[0].rearrange("p n t -> p (n t)").bitcast(I32)
        nc.sync.dma_start(out=word_rows[:, :HALF], in_=o_codes[:, :HALF].bitcast(I32))
        for u in range(2):
            copy_on("scalar", o_sb[1][:, 2 * u : 2 * u + 2, :], banks1[u][:])
        nc.scalar.dma_start(out=out_rows[:, :, HALF:], in_=o_sb[1][:])
        for lo in quarters:
            src, dst = weave(o_sb[1][:, :, lo : lo + QUARTER], o_b[1, lo][:])
            copy_on("vector", dst, src)
        for lo in quarters:
            quantize_out(1, lo, QUARTER)
        nc.sync.dma_start(out=word_rows[:, HALF:], in_=o_codes[:, HALF:].bitcast(I32))
        for q in range(P // QUADRANT):
            queue = nc.sync if q < 2 else nc.scalar
            queue.dma_start(
                out=out_2[0, PACK * q : PACK * (q + 1), :].bitcast(I32),
                in_=o_scales[QUADRANT * q : QUADRANT * q + PACK, :].bitcast(I32),
            )
